import numpy as np
import ml_dtypes


def mxq(x, axis, fmt="e4m3"):
    dtype, down = {"e4m3": (ml_dtypes.float8_e4m3fn, 7), "e5m2": (ml_dtypes.float8_e5m2, 14)}[fmt]
    v = np.moveaxis(np.asarray(x, np.float32).astype(ml_dtypes.bfloat16).astype(np.float64), axis, -1)
    blocks = v.reshape(v.shape[:-1] + (-1, 32))
    amax = np.abs(blocks).max(-1, keepdims=True)
    byte = np.maximum(np.where(amax > 0, np.frexp(amax)[1] - 1 + 127, 0) - down, 1)
    scale = np.exp2(byte - 127.0)
    codes = (blocks / scale).astype(np.float32).astype(dtype).astype(np.float64)
    return np.moveaxis((codes * scale).reshape(v.shape), -1, axis)


WIDE = False


def mx_kscale(k):
    if not WIDE:
        return np.ones(k)
    levels = np.array([10, -10, 5, -5, 0])
    if k % 512:
        return np.exp2(np.random.permutation(np.resize(levels, k // 32))).repeat(32)
    a = np.empty((k // 512, 16))
    for p in range(k // 512):
        a[p, :8] = np.random.permutation(np.resize(levels, 8))
        for g in range(8):
            far = levels[np.abs(levels - a[p, g]) >= 10]
            a[p, g + 8] = far[np.random.randint(len(far))]
    return np.exp2(a.ravel()).repeat(32)


def f64(x):
    return np.asarray(x).astype(np.float64)


def striped(idx):
    return np.tile(idx.reshape(-1, 16).T, (8, 1)).astype(np.uint16)


def unstriped(offs):
    return offs[:16].T.reshape(-1).astype(np.int64)


def pack_weight(w):
    k, n = w.shape
    w = f64(np.asarray(w, np.float32).astype(ml_dtypes.bfloat16)).reshape(k // 32, 32, n)
    amax = np.abs(w).max(1)
    byte = np.clip(np.where(amax > 0, np.frexp(amax)[1] - 1 + 127 - 7, 1), 1, 254)
    scaled = (w * np.exp2(127.0 - byte)[:, None, :]).reshape(k, n).astype(np.float32)
    words = np.ascontiguousarray(scaled.reshape(k // 512, 128, 4, n).transpose(0, 1, 3, 2)).astype(ml_dtypes.float8_e4m3fn).view(np.uint8)
    return words, np.ascontiguousarray(byte.astype(np.uint8).reshape(k // 512, 16, n))


def unpack_weight(words, scales):
    g, p, n, _ = words.shape
    vals = np.ascontiguousarray(words).view(ml_dtypes.float8_e4m3fn).astype(np.float64) * np.repeat(np.exp2(scales.astype(np.float64) - 127.0), 8, axis=1)[..., None]
    return vals.transpose(0, 1, 3, 2).reshape(g * 512, n)


E2M1 = np.array([0.0, 0.5, 1.0, 1.5, 2.0, 3.0, 4.0, 6.0, -0.0, -0.5, -1.0, -1.5, -2.0, -3.0, -4.0, -6.0])


def pack_fp4(w):
    k, n = w.shape
    w = f64(np.asarray(w, np.float32).astype(ml_dtypes.bfloat16)).reshape(k // 32, 32, n)
    amax = np.abs(w).max(1)
    mant, ex = np.frexp(amax / 6.0)
    byte = np.clip(np.where(amax > 0, np.where(mant > 0.5, ex, ex - 1) + 127, 1), 1, 254)
    scaled = (w * np.exp2(127.0 - byte)[:, None, :]).reshape(k, n).astype(np.float32)
    c = np.ascontiguousarray(scaled.reshape(k // 512, 128, 4, n).transpose(0, 1, 3, 2)).astype(ml_dtypes.float4_e2m1fn).view(np.uint8) & 0xF
    words = (c[..., 0::2] | (c[..., 1::2] << 4)).reshape(k // 512, 128, 2 * n)
    return np.ascontiguousarray(words), np.ascontiguousarray(byte.astype(np.uint8).reshape(k // 512, 16, n))


def unpack_fp4(words, scales):
    g, _, n = scales.shape
    words = np.ascontiguousarray(words).reshape(g, 128, n, 2)
    nib = np.empty((g, 128, n, 4), np.uint8)
    nib[..., 0::2] = words & 0xF
    nib[..., 1::2] = words >> 4
    vals = E2M1[nib] * np.repeat(np.exp2(scales.astype(np.float64) - 127.0), 8, axis=1)[..., None]
    return vals.transpose(0, 1, 3, 2).reshape(g * 512, n)


K, T, S, N, H = 1024, 1024, 512, 256, 512


def setup_inputs():
    n = np.random.standard_normal
    s = mx_kscale(K)[:, None]
    u = mx_kscale(H)
    packed_xT = pack_weight(n((K, T)) * s)
    packed_w1 = pack_fp4(n((K, H)) / np.sqrt(K) / s)
    packed_w2 = pack_fp4(n((K, H)) / np.sqrt(K) / s)
    packed_w3 = pack_fp4(n((K, H)) / np.sqrt(K) / s)
    packed_w4 = pack_fp4(n((H, N)) / np.sqrt(H) / u[:, None])
    return {
        "x_words": packed_xT[0],
        "x_scales": packed_xT[1],
        "w1_words": packed_w1[0],
        "w1_scales": packed_w1[1],
        "w2_words": packed_w2[0],
        "w2_scales": packed_w2[1],
        "w3_words": packed_w3[0],
        "w3_scales": packed_w3[1],
        "lame": (np.random.uniform(0.6, 1.4, (H, 1))).astype(np.float32),
        "cubw": (np.random.uniform(0.5, 1.5, (H, S))).astype(np.float32),
        "unit": (np.random.uniform(0.6, 1.4, (H, 1)) * u[:, None]).astype(np.float32),
        "w4_words": packed_w4[0],
        "w4_scales": packed_w4[1],
        "offs": striped(np.random.permutation(T)[:S]),
        "opp": striped(np.random.permutation(S)),
    }


def reference(x_words, x_scales, w1_words, w1_scales, w2_words, w2_scales, w3_words, w3_scales, lame, cubw, unit, w4_words, w4_scales, offs, opp):
    xq = unpack_weight(x_words, x_scales)[:, unstriped(offs)]
    fxx = unpack_fp4(w1_words, w1_scales).T @ xq
    da = 0.5 * np.tanh(fxx) + 1.0
    fxy = unpack_fp4(w2_words, w2_scales).T @ xq
    de = 0.5 * np.tanh(fxy)
    exx = 0.5 * ((da) ** 2 + (de) ** 2) - 0.5
    fyy = unpack_fp4(w3_words, w3_scales).T @ xq
    dg = 0.5 * np.tanh(fyy) + 1.0
    eyy = 0.5 * ((dg) ** 2 + (de) ** 2) - 0.5
    sxx = f64(lame) * (exx + eyy) + 2.0 * exx
    exy = 0.5 * (de * (da + dg))
    pxx = da * sxx + de * (2.0 * exy)
    eo = exy[:, unstriped(opp)]
    hid = f64(unit) * (pxx * f64(cubw) - eo)
    return unpack_fp4(w4_words, w4_scales).T @ mxq(hid, 0, "e4m3")

@@ -1,0 +1,283 @@
+from contextlib import ExitStack
+
+import concourse.mybir as mybir
+from concourse.masks import make_identity
+
+K, T, S, N, H = 1024, 1024, 512, 256, 512
+FLOPS = 2 * (3 * K * H * S + H * N * S)
+
+F32 = mybir.dt.float32
+BF16 = mybir.dt.bfloat16
+I32 = mybir.dt.int32
+U32 = mybir.dt.uint32
+U16 = mybir.dt.uint16
+U8 = mybir.dt.uint8
+FP8X4 = mybir.dt.float8_e4m3fn_x4
+FP4X4 = mybir.dt.float4_e2m1fn_x4
+ACT = mybir.ActivationFunctionType
+ADD = mybir.AluOpType.add
+SUB = mybir.AluOpType.subtract
+MULT = mybir.AluOpType.mult
+
+P = 128
+PACK = 4
+PASSES = K // (P * PACK)
+BLOCKS = S // P
+LIST_COLS = P // 16
+
+
+def load_scale_rows(queue, plane, scales):
+    rows = scales.bitcast(I32).rearrange("o (q r) c -> r q o c", r=4)
+    for r in range(4):
+        queue.dma_start(out=plane.bitcast(I32)[r:P:32, :, :], in_=rows[r])
+
+
+def tile_picked_ystvkf_shear_p_kernel(
+    tc, x_words, x_scales, w1_words, w1_scales, w2_words, w2_scales, w3_words, w3_scales,
+    lame, cubw, unit, w4_words, w4_scales, offs, opp, out,
+):
+    nc = tc.nc
+    with ExitStack() as ctx:
+        held = ctx.enter_context(tc.tile_pool(name="held", bufs=1))
+        psum = ctx.enter_context(tc.psum_pool(name="psum", bufs=1))
+
+        offs_sb = held.tile([P, S // 16], U16, name="offs_sb")
+        opp_sb = held.tile([P, S // 16], U16, name="opp_sb")
+        xs_all = held.tile([P, PASSES, T], U8, name="xs_all", align_bytes=64)
+        xw_all = [held.tile([P, T], U32, name=f"xw_all{o}", align_bytes=64) for o in range(PASSES)]
+        ww = [held.tile([P, PASSES, 2 * H], U8, name=f"ww{i}", align_bytes=64) for i in range(3)]
+        ws = [held.tile([P, PASSES, H], U8, name=f"ws{i}", align_bytes=64) for i in range(3)]
+        w4w = held.tile([P, 2 * N], U8, name="w4w", align_bytes=64)
+        w4s = held.tile([P, 1, N], U8, name="w4s", align_bytes=64)
+        lam = held.tile([P, PACK], F32, name="lam")
+        uni = held.tile([P, PACK], F32, name="uni")
+        cub = held.tile([P, PACK, S], F32, name="cub")
+        ident = held.tile([P, P], F32, name="ident")
+
+        w_words = (w1_words, w3_words, w2_words)
+        w_scales = (w1_scales, w3_scales, w2_scales)
+
+        nc.gpsimd.memset(xs_all[:].bitcast(I32), 0)
+        for i in range(3):
+            nc.vector.memset(ws[i][:].bitcast(I32), 0)
+        nc.vector.memset(w4s[:].bitcast(I32), 0)
+
+        def load_words(i):
+            nc.sync.dma_start(out=ww[i][:].bitcast(I32), in_=w_words[i].bitcast(I32).rearrange("o p c -> p o c"))
+
+        def load_x(o):
+            nc.sync.dma_start(out=xw_all[o][:].bitcast(I32),
+                              in_=x_words[o].rearrange("p c r -> p (c r)").bitcast(I32))
+
+        nc.sync.dma_start(offs_sb[:], offs)
+        load_scale_rows(nc.sync, xs_all[:], x_scales)
+        load_x(0)
+        nc.sync.dma_start(out=uni[:], in_=unit.rearrange("(p t) o -> p (t o)", t=PACK))
+        nc.sync.dma_start(out=lam[:], in_=lame.rearrange("(p t) o -> p (t o)", t=PACK))
+        load_x(1)
+        load_words(0)
+        load_scale_rows(nc.sync, ws[0][:], w_scales[0])
+        load_words(1)
+        load_words(2)
+        load_scale_rows(nc.gpsimd, ws[2][:], w_scales[2])
+        load_scale_rows(nc.sync, ws[1][:], w_scales[1])
+        nc.sync.dma_start(out=cub[:], in_=cubw.rearrange("(p t) j -> p t j", t=PACK))
+        nc.sync.dma_start(opp_sb[:], opp)
+        nc.sync.dma_start(out=w4w[:].bitcast(I32), in_=w4_words[0].bitcast(I32))
+        load_scale_rows(nc.sync, w4s[:], w4_scales)
+        make_identity(nc, ident[:])
+
+        c_e = held.tile([P, PACK], F32, name="c_e")
+        nc.gpsimd.tensor_scalar(c_e[:], uni[:], -0.125, 0.0, MULT, ADD)
+        c_b = held.tile([P, PACK], F32, name="c_b")
+        nc.gpsimd.tensor_scalar(c_b[:], uni[:], -0.5, 0.0, MULT, ADD)
+        coef = []
+        for name, mul, add in (("c_n", 0.0625, 0.125), ("c_m", 0.0625, 0.0), ("c_0", -0.5, -0.5), ("c_0a", -0.25, 0.0), ("c_0g", -0.25, -0.5), ("c_ee", 0.125, 0.125), ("c_0ag", 0.0, 0.0)):
+            lin = held.tile([P, PACK], F32, name=name + "_lin")
+            nc.gpsimd.tensor_scalar(lin[:], lam[:], mul, add, MULT, ADD)
+            c = held.tile([P, PACK], F32, name=name)
+            nc.gpsimd.tensor_tensor(c[:], lin[:], uni[:], MULT)
+            coef.append(c)
+        c_n, c_m, c_0, c_0a, c_0g, c_ee, c_0ag = coef
+
+        xw, xs = {}, {}
+        shear = [held.tile([P, S], F32, name=f"shear{t}") for t in range(PACK)]
+
+        def work(name, b):
+            return held.tile([P, PACK, P], F32, name=f"{name}{b}")
+
+        def gather_points(b):
+            picks = offs_sb[:, b * LIST_COLS:(b + 1) * LIST_COLS]
+            for o in range(PASSES):
+                xs[o, b] = held.tile([P, P], U8, name=f"xs{o}", bufs=4, align_bytes=64)
+                xw[o, b] = held.tile([P, P], U32, name=f"xw{o}", bufs=2, align_bytes=64)
+                nc.vector.tensor_copy(xs[o, b][:], xs_all[:, o, :].indirect(picks))
+                nc.vector.tensor_copy(xw[o, b][:], xw_all[o][:].indirect(picks))
+
+        def turn(bank, terms):
+            for n, term in enumerate(terms):
+                for t in range(PACK):
+                    nc.tensor.matmul(bank[:, t, :], term[:, t, :], ident[:], is_transpose=True,
+                                     start=(n == 0 and t == 0), stop=(n == len(terms) - 1 and t == PACK - 1))
+
+        out_v = out.rearrange("(h p) j -> p h j", p=P)
+        v = {}
+        vsq = {}
+
+        def cols_of(b):
+            return slice(b * P, (b + 1) * P)
+
+        def two(eng):
+            return nc.gpsimd if eng == "g" else nc.vector
+
+        def step(name, b, eng):
+            cols = cols_of(b)
+            picks = opp_sb[:, b * LIST_COLS:(b + 1) * LIST_COLS]
+            if name == "G":
+                gather_points(b)
+            elif name in ("Ma", "Mg", "Me"):
+                i = "age".index(name[1])
+                pre = psum.tile([P, H], F32, name=f"pre{i}")
+                for o in range(PASSES):
+                    nc.tensor.matmul_mx(pre[:], lhsT=xw[o, b][:].bitcast(FP8X4), lhsT_scale=xs[o, b][:],
+                                        rhs=ww[i][:, o, :].bitcast(FP4X4), rhs_scale=ws[i][:, o, :],
+                                        start=(o == 0), stop=(o == PASSES - 1))
+                v["pre" + name[1], b] = pre
+            elif name in ("Ta", "Tg", "Te"):
+                y = work("th_" + name[1], b)
+                nc.scalar.activation(y[:], v["pre" + name[1], b][:].rearrange("p (m t) -> p t m", t=PACK), ACT.Tanh)
+                v[name[1], b] = y
+            elif name in ("Qa", "Qg", "Qe"):
+                src = v[name[1], b]
+                dst = work("sq_" + name[1], b)
+                shift = 0.0 if name == "Qe" else 2.0
+                if eng == "s":
+                    nc.scalar.activation(dst[:], src[:], ACT.Square, scale=1.0, bias=shift)
+                elif name == "Qe":
+                    two(eng).tensor_tensor(dst[:], src[:], src[:], MULT)
+                else:
+                    nc.vector.scalar_tensor_tensor(dst[:], src[:], 4.0, src[:], ADD, MULT)
+                    vsq[name[1], b] = True
+                v[name[1] + "2", b] = dst
+            elif name[0] == "H":
+                terms = {"s": ("a", "g"), "e": ("e",), "m": ("e2", "g2"), "n": ("e2", "a2"), "a": ("a",), "g": ("g",)}[name[1]]
+                tag = {"m": "g", "n": "a"}.get(name[1], name[1])
+                bank = psum.tile([P, PACK, P], F32, name="b_" + tag, bufs=2 if tag == "a" else 1)
+                turn(bank, [v[x, b] for x in terms])
+                v["b_" + name[1], b] = bank
+            elif name == "sF":
+                s_f = work("s_f", b)
+                for t in range(PACK):
+                    nc.scalar.activation(s_f[:, t, :], v["b_s", b][:, t, :], ACT.Identity,
+                                         scale=c_e[:, t:t + 1], bias=c_b[:, t:t + 1])
+                v["s_f", b] = s_f
+            elif name == "X":
+                for t in range(PACK):
+                    nc.vector.tensor_tensor(shear[t][:, cols], v["b_e", b][:, t, :], v["s_f", b][:, t, :], MULT)
+            elif name == "D":
+                d = work("d", b)
+                for t in range(PACK):
+                    nc.vector.tensor_tensor(d[:, t, :], v["b_e", b][:, t, :], shear[t][:, cols], MULT)
+                v["d", b] = d
+            elif name == "mF":
+                m_f = work("m_f", b)
+                c0 = {(False, False): c_0, (True, False): c_0a, (False, True): c_0g, (True, True): c_0ag}[
+                    vsq.get(("a", b), False), vsq.get(("g", b), False)]
+                for t in range(PACK):
+                    nc.scalar.activation(m_f[:, t, :], v["b_m", b][:, t, :], ACT.Identity,
+                                         scale=c_m[:, t:t + 1], bias=c0[:, t:t + 1])
+                v["m_f", b] = m_f
+            elif name == "sx":
+                sx = work("sx", b)
+                for t in range(PACK):
+                    nc.vector.scalar_tensor_tensor(sx[:, t, :], v["b_n", b][:, t, :], c_n[:, t:t + 1],
+                                                   v["m_f", b][:, t, :], MULT, ADD)
+                v["sx", b] = sx
+            elif name in ("Fa", "Fg", "Fe"):
+                dst = work("sq_" + name[1], b)
+                nc.scalar.activation(dst[:], v["b_" + name[1], b][:], ACT.Square, scale=1.0,
+                                     bias=0.0 if name == "Fe" else 2.0)
+                v[name[1] + "2", b] = dst
+            elif name == "ak":
+                dst = work("ak", b)
+                for t in range(PACK):
+                    if eng == "s":
+                        nc.scalar.activation(dst[:, t, :], v["a2", b][:, t, :], ACT.Identity,
+                                             scale=c_n[:, t:t + 1], bias=c_0[:, t:t + 1])
+                    else:
+                        two(eng).tensor_scalar(dst[:, t, :], v["a2", b][:, t, :], c_n[:, t:t + 1], c_0[:, t:t + 1], MULT, ADD)
+                v["ak", b] = dst
+            elif name == "y":
+                dst = work("y", b)
+                for t in range(PACK):
+                    nc.vector.scalar_tensor_tensor(dst[:, t, :], v["g2", b][:, t, :], c_m[:, t:t + 1],
+                                                   v["ak", b][:, t, :], MULT, ADD)
+                v["y", b] = dst
+            elif name == "sy":
+                dst = work("sx", b)
+                for t in range(PACK):
+                    nc.vector.scalar_tensor_tensor(dst[:, t, :], v["e2", b][:, t, :], c_ee[:, t:t + 1],
+                                                   v["y", b][:, t, :], MULT, ADD)
+                v["sx", b] = dst
+            elif name == "D2":
+                d = work("d", b)
+                nc.vector.tensor_tensor(d[:], v["e2", b][:], v["s_f", b][:], MULT)
+                v["d", b] = d
+            elif name == "AR":
+                ar = work("ar", b)
+                nc.vector.scalar_tensor_tensor(ar[:], v["b_a", b][:], 2.0, v["sx", b][:], ADD, MULT)
+                v["ar", b] = ar
+            elif name == "P":
+                pxx = work("pxx", b)
+                two(eng).tensor_tensor(pxx[:], v["ar", b][:], v["d", b][:], SUB)
+                v["pxx", b] = pxx
+            elif name == "Pc":
+                pc = work("pc", b)
+                two(eng).tensor_tensor(pc[:], v["pxx", b][:], cub[:, :, cols], MULT)
+                v["pc", b] = pc
+            elif name == "E":
+                eo = work("eo", b)
+                for t in range(PACK):
+                    if eng == "s":
+                        nc.scalar.activation(eo[:, t, :], shear[t][:].indirect(picks), ACT.Copy)
+                    else:
+                        nc.vector.tensor_copy(eo[:, t, :], shear[t][:].indirect(picks))
+                v["eo", b] = eo
+            elif name == "ga":
+                hid = work("hid", b)
+                if ("eo", b) in v:
+                    two(eng).tensor_tensor(hid[:], v["eo", b][:], v["pc", b][:], ADD)
+                else:
+                    for t in range(PACK):
+                        nc.vector.tensor_tensor(hid[:, t, :], shear[t][:].indirect(picks), v["pc", b][:, t, :], ADD)
+                v["hid", b] = hid
+            elif name == "il":
+                hb = held.tile([P, P, PACK], BF16, name=f"hb{b}", align_bytes=64)
+                dst = hb[:].rearrange("p (c i) t -> p c t i", i=4)
+                src = v["hid", b][:].rearrange("p t (c i) -> p c t i", i=4)
+                if eng == "s":
+                    nc.scalar.copy(dst, src)
+                else:
+                    nc.vector.tensor_copy(dst, src)
+                v["hb", b] = hb
+            elif name == "q":
+                hw = held.tile([P, P], U32, name=f"hw{b}", align_bytes=64)
+                hs = held.tile([P, P], U8, name=f"hs{b}", align_bytes=64)
+                nc.vector.quantize_mx(hw[:].bitcast(FP8X4), hs[:], v["hb", b][:].rearrange("p c t -> p (c t)"))
+                acc = psum.tile([P, N // P, P], F32, name=f"pre{b % 3}")
+                for h in range(N // P):
+                    nc.tensor.matmul_mx(acc[:, h, :], lhsT=w4w[:, 2 * P * h:2 * P * (h + 1)].bitcast(FP4X4),
+                                        lhsT_scale=w4s[:, 0, P * h:P * (h + 1)],
+                                        rhs=hw[:].bitcast(FP8X4), rhs_scale=hs[:], start=True, stop=True)
+                v["acc", b] = acc
+            elif name == "o":
+                res = held.tile([P, N // P, P], F32, name=f"res{b}")
+                if eng == "s":
+                    nc.scalar.copy(res[:], v["acc", b][:])
+                else:
+                    nc.vector.tensor_copy(res[:], v["acc", b][:])
+                nc.sync.dma_start(out=out_v[:, :, cols], in_=res[:])
+
+        for word in "G.0.v Ma.0.p Mg.0.p Me.0.p G.1.v Ta.0.s Tg.0.s Te.0.s Hs.0.p He.0.p Ha.0.p Hg.0.p Ma.1.p Mg.1.p Me.1.p G.2.v G.3.v sF.0.s Fe.0.s X.0.v D2.0.v Ta.1.s Tg.1.s Te.1.s Hs.1.p He.1.p Ma.2.p Mg.2.p Me.2.p Fa.0.s ak.0.v Fg.0.s y.0.v sy.0.v AR.0.v Ha.1.p Hg.1.p sF.1.s Fe.1.s X.1.v D2.1.v P.0.v Pc.0.v Ta.2.s Tg.2.s Te.2.s Hs.2.p He.2.p Ma.3.p Mg.3.p Me.3.p Fa.1.s ak.1.v Fg.1.s y.1.v sy.1.v AR.1.v Ha.2.p Hg.2.p sF.2.s Fe.2.s X.2.v D2.2.v P.1.v Pc.1.v Ta.3.s Tg.3.s Te.3.s Hs.3.p He.3.p Fa.2.s ak.2.s Fg.2.s y.2.v sy.2.v AR.2.v Ha.3.p Hg.3.p sF.3.s Fe.3.s X.3.v D2.3.v P.2.v Pc.2.v ga.0.v il.0.s q.0.v o.0.s Fa.3.s ak.3.s Fg.3.s y.3.v sy.3.v AR.3.v E.3.s E.1.s ga.1.v il.1.s q.1.v o.1.s P.3.v Pc.3.v E.2.s ga.2.v il.2.s q.2.v o.2.s ga.3.v il.3.v q.3.v o.3.s".split():
+            name, b, eng = word.split(".")
+            step(name, int(b), eng)

@@ -26,9 +26,9 @@ BLOCKS = S // P
 LIST_COLS = P // 16
 
 
-def load_scale_rows(queue, plane, scales):
+def load_scale_rows(queue, plane, scales, which=range(4)):
     rows = scales.bitcast(I32).rearrange("o (q r) c -> r q o c", r=4)
-    for r in range(4):
+    for r in which:
         queue.dma_start(out=plane.bitcast(I32)[r:P:32, :, :], in_=rows[r])
 
 
@@ -44,7 +44,7 @@ def tile_picked_ystvkf_shear_p_kernel(
         offs_sb = held.tile([P, S // 16], U16, name="offs_sb")
         opp_sb = held.tile([P, S // 16], U16, name="opp_sb")
         xs_all = held.tile([P, PASSES, T], U8, name="xs_all", align_bytes=64)
-        xw_all = [held.tile([P, T], U32, name=f"xw_all{o}", align_bytes=64) for o in range(PASSES)]
+        xw_all = held.tile([P, PASSES, T], U32, name="xw_all", align_bytes=64)
         ww = [held.tile([P, PASSES, 2 * H], U8, name=f"ww{i}", align_bytes=64) for i in range(3)]
         ws = [held.tile([P, PASSES, H], U8, name=f"ws{i}", align_bytes=64) for i in range(3)]
         w4w = held.tile([P, 2 * N], U8, name="w4w", align_bytes=64)
@@ -56,6 +56,7 @@ def tile_picked_ystvkf_shear_p_kernel(
 
         w_words = (w1_words, w3_words, w2_words)
         w_scales = (w1_scales, w3_scales, w2_scales)
+        ORD = "age"
 
         nc.gpsimd.memset(xs_all[:].bitcast(I32), 0)
         for i in range(3):
@@ -66,218 +67,231 @@ def tile_picked_ystvkf_shear_p_kernel(
             nc.sync.dma_start(out=ww[i][:].bitcast(I32), in_=w_words[i].bitcast(I32).rearrange("o p c -> p o c"))
 
         def load_x(o):
-            nc.sync.dma_start(out=xw_all[o][:].bitcast(I32),
-                              in_=x_words[o].rearrange("p c r -> p (c r)").bitcast(I32))
+            nc.sync.dma_start(out=xw_all[:].bitcast(I32),
+                              in_=x_words.rearrange("o p c r -> p o (c r)").bitcast(I32))
 
         nc.sync.dma_start(offs_sb[:], offs)
         load_scale_rows(nc.sync, xs_all[:], x_scales)
-        load_x(0)
         nc.sync.dma_start(out=uni[:], in_=unit.rearrange("(p t) o -> p (t o)", t=PACK))
         nc.sync.dma_start(out=lam[:], in_=lame.rearrange("(p t) o -> p (t o)", t=PACK))
-        load_x(1)
-        load_words(0)
+        load_x(0)
         load_scale_rows(nc.sync, ws[0][:], w_scales[0])
+        load_words(0)
         load_words(1)
         load_words(2)
-        load_scale_rows(nc.gpsimd, ws[2][:], w_scales[2])
         load_scale_rows(nc.sync, ws[1][:], w_scales[1])
+        load_scale_rows(nc.gpsimd, ws[2][:], w_scales[2])
         nc.sync.dma_start(out=cub[:], in_=cubw.rearrange("(p t) j -> p t j", t=PACK))
         nc.sync.dma_start(opp_sb[:], opp)
         nc.sync.dma_start(out=w4w[:].bitcast(I32), in_=w4_words[0].bitcast(I32))
         load_scale_rows(nc.sync, w4s[:], w4_scales)
         make_identity(nc, ident[:])
 
-        c_e = held.tile([P, PACK], F32, name="c_e")
-        nc.gpsimd.tensor_scalar(c_e[:], uni[:], -0.125, 0.0, MULT, ADD)
-        c_b = held.tile([P, PACK], F32, name="c_b")
-        nc.gpsimd.tensor_scalar(c_b[:], uni[:], -0.5, 0.0, MULT, ADD)
-        coef = []
-        for name, mul, add in (("c_n", 0.0625, 0.125), ("c_m", 0.0625, 0.0), ("c_0", -0.5, -0.5), ("c_0a", -0.25, 0.0), ("c_0g", -0.25, -0.5), ("c_ee", 0.125, 0.125), ("c_0ag", 0.0, 0.0)):
-            lin = held.tile([P, PACK], F32, name=name + "_lin")
-            nc.gpsimd.tensor_scalar(lin[:], lam[:], mul, add, MULT, ADD)
-            c = held.tile([P, PACK], F32, name=name)
-            nc.gpsimd.tensor_tensor(c[:], lin[:], uni[:], MULT)
-            coef.append(c)
-        c_n, c_m, c_0, c_0a, c_0g, c_ee, c_0ag = coef
+        ce = nc.gpsimd
+        LINES = ((0.0, -0.125), (0.0, -0.5), (0.0625, 0.0), (0.0625, 0.125), (0.125, 0.125), (-0.5, -0.5))
+        lin = held.tile([P, len(LINES), PACK], F32, name="lin")
+        coef = held.tile([P, len(LINES), PACK], F32, name="coef")
+        for n, (slope, offset) in enumerate(LINES):
+            if slope == 0.0:
+                ce.memset(lin[:, n, :], offset)
+            else:
+                ce.tensor_scalar(lin[:, n, :], lam[:], slope, offset, MULT, ADD)
+        ce.tensor_tensor(coef[:], lin[:], uni[:].unsqueeze(1).to_broadcast([P, len(LINES), PACK]), MULT)
+        c_e, c_b, c_m, c_n, c_ee, c_0 = (coef[:, n, :] for n in range(len(LINES)))
 
-        xw, xs = {}, {}
-        shear = [held.tile([P, S], F32, name=f"shear{t}") for t in range(PACK)]
-
-        def work(name, b):
-            return held.tile([P, PACK, P], F32, name=f"{name}{b}")
-
-        def gather_points(b):
-            picks = offs_sb[:, b * LIST_COLS:(b + 1) * LIST_COLS]
-            for o in range(PASSES):
-                xs[o, b] = held.tile([P, P], U8, name=f"xs{o}", bufs=4, align_bytes=64)
-                xw[o, b] = held.tile([P, P], U32, name=f"xw{o}", bufs=2, align_bytes=64)
-                nc.vector.tensor_copy(xs[o, b][:], xs_all[:, o, :].indirect(picks))
-                nc.vector.tensor_copy(xw[o, b][:], xw_all[o][:].indirect(picks))
-
-        def turn(bank, terms):
-            for n, term in enumerate(terms):
-                for t in range(PACK):
-                    nc.tensor.matmul(bank[:, t, :], term[:, t, :], ident[:], is_transpose=True,
-                                     start=(n == 0 and t == 0), stop=(n == len(terms) - 1 and t == PACK - 1))
-
+        xs = [held.tile([P, S], U8, name=f"xs{o}", align_bytes=64) for o in range(PASSES)]
+        xw = {}
+        shear_all = held.tile([P, PACK, S], F32, name="shear")
+        shear = [shear_all[:, t, :] for t in range(PACK)]
         out_v = out.rearrange("(h p) j -> p h j", p=P)
+        W = 2 * P
         v = {}
         vsq = {}
+        force = held.tile([P, PACK, S], F32, name="force")
+        opp_val = held.tile([P, PACK, S], F32, name="eo")
+        UNITS = [[[0],[0,1,2,3]],[[1],[0,1,2,3]],[[2],[0,1,2,3]],[[3],[0,1,2,3]]]
 
-        def cols_of(b):
-            return slice(b * P, (b + 1) * P)
+        def twork(name, b):
+            return held.tile([P, PACK, P], F32, name=f"{name}{b}")
 
-        def two(eng):
-            return nc.gpsimd if eng == "g" else nc.vector
+        def fwork(name, u):
+            return held.tile([P, len(UNITS[u][1]), P * len(UNITS[u][0])], F32, name=f"{name}{u}")
 
-        def step(name, b, eng):
-            cols = cols_of(b)
-            picks = opp_sb[:, b * LIST_COLS:(b + 1) * LIST_COLS]
-            if name == "G":
-                gather_points(b)
-            elif name in ("Ma", "Mg", "Me"):
-                i = "age".index(name[1])
-                pre = psum.tile([P, H], F32, name=f"pre{i}")
+        def step(name, i, eng):
+            blks, ts = UNITS[i]
+            gcols = slice(blks[0] * P, (blks[-1] + 1) * P)
+            pair = list(enumerate(ts))
+            trange = slice(ts[0], ts[-1] + 1)
+            cols = slice(i * P, (i + 1) * P)
+            if name == "Gs":
+                n = S // 2
                 for o in range(PASSES):
-                    nc.tensor.matmul_mx(pre[:], lhsT=xw[o, b][:].bitcast(FP8X4), lhsT_scale=xs[o, b][:],
-                                        rhs=ww[i][:, o, :].bitcast(FP4X4), rhs_scale=ws[i][:, o, :],
+                    nc.vector.tensor_copy(xs[o][:, i * n:(i + 1) * n], xs_all[:, o, :].indirect(offs_sb[:, i * n // 16:(i + 1) * n // 16]))
+            elif name == "G":
+                for o in range(PASSES):
+                    xw[o, i] = held.tile([P, P], U32, name=f"xw{o}", bufs=4, align_bytes=64)
+                    nc.vector.tensor_copy(xw[o, i][:], xw_all[:, o, :].indirect(offs_sb[:, i * LIST_COLS:(i + 1) * LIST_COLS]))
+            elif name in ("Ma", "Mg", "Me"):
+                k = ORD.index(name[1])
+                pre = psum.tile([P, H], F32, name="pre", bufs=3)
+                for o in range(PASSES):
+                    nc.tensor.matmul_mx(pre[:], lhsT=xw[o, i][:].bitcast(FP8X4), lhsT_scale=xs[o][:, cols],
+                                        rhs=ww[k][:, o, :].bitcast(FP4X4), rhs_scale=ws[k][:, o, :],
                                         start=(o == 0), stop=(o == PASSES - 1))
-                v["pre" + name[1], b] = pre
+                v["pre" + name[1], i] = pre
             elif name in ("Ta", "Tg", "Te"):
-                y = work("th_" + name[1], b)
-                nc.scalar.activation(y[:], v["pre" + name[1], b][:].rearrange("p (m t) -> p t m", t=PACK), ACT.Tanh)
-                v[name[1], b] = y
+                y = twork("th_" + name[1], i)
+                nc.scalar.activation(y[:], v["pre" + name[1], i][:].rearrange("p (m t) -> p t m", t=PACK), ACT.Tanh)
+                v[name[1], i] = y
             elif name in ("Qa", "Qg", "Qe"):
-                src = v[name[1], b]
-                dst = work("sq_" + name[1], b)
-                shift = 0.0 if name == "Qe" else 2.0
-                if eng == "s":
-                    nc.scalar.activation(dst[:], src[:], ACT.Square, scale=1.0, bias=shift)
+                src = v[name[1], i]
+                dst = twork("sq_" + name[1], i)
+                if name == "Qe" and eng == "s":
+                    nc.scalar.activation(dst[:], src[:], ACT.Square)
                 elif name == "Qe":
-                    two(eng).tensor_tensor(dst[:], src[:], src[:], MULT)
+                    nc.vector.tensor_tensor(dst[:], src[:], src[:], MULT)
+                elif eng == "s":
+                    nc.scalar.activation(dst[:], src[:], ACT.Square, scale=1.0, bias=2.0)
+                    vsq[i] = True
                 else:
                     nc.vector.scalar_tensor_tensor(dst[:], src[:], 4.0, src[:], ADD, MULT)
-                    vsq[name[1], b] = True
-                v[name[1] + "2", b] = dst
+                v[name[1] + "2", i] = dst
             elif name[0] == "H":
                 terms = {"s": ("a", "g"), "e": ("e",), "m": ("e2", "g2"), "n": ("e2", "a2"), "a": ("a",), "g": ("g",)}[name[1]]
                 tag = {"m": "g", "n": "a"}.get(name[1], name[1])
-                bank = psum.tile([P, PACK, P], F32, name="b_" + tag, bufs=2 if tag == "a" else 1)
-                turn(bank, [v[x, b] for x in terms])
-                v["b_" + name[1], b] = bank
+                bank = psum.tile([P, len(ts), P * len(blks)], F32, name="b_" + tag, bufs={"a":2,"e":1,"g":1,"s":1}[tag])
+                moves = [(x, bb, tt, t) for bb in range(len(blks)) for x in terms for tt, t in pair]
+                for n, (x, bb, tt, t) in enumerate(moves):
+                    nc.tensor.matmul(bank[:, tt, bb * P:(bb + 1) * P], v[x, blks[bb]][:, t, :], ident[:],
+                                     is_transpose=True, start=(n == 0), stop=(n == len(moves) - 1))
+                v["b_" + name[1], i] = bank
             elif name == "sF":
-                s_f = work("s_f", b)
-                for t in range(PACK):
-                    nc.scalar.activation(s_f[:, t, :], v["b_s", b][:, t, :], ACT.Identity,
-                                         scale=c_e[:, t:t + 1], bias=c_b[:, t:t + 1])
-                v["s_f", b] = s_f
-            elif name == "X":
-                for t in range(PACK):
-                    nc.vector.tensor_tensor(shear[t][:, cols], v["b_e", b][:, t, :], v["s_f", b][:, t, :], MULT)
-            elif name == "D":
-                d = work("d", b)
-                for t in range(PACK):
-                    nc.vector.tensor_tensor(d[:, t, :], v["b_e", b][:, t, :], shear[t][:, cols], MULT)
-                v["d", b] = d
-            elif name == "mF":
-                m_f = work("m_f", b)
-                c0 = {(False, False): c_0, (True, False): c_0a, (False, True): c_0g, (True, True): c_0ag}[
-                    vsq.get(("a", b), False), vsq.get(("g", b), False)]
-                for t in range(PACK):
-                    nc.scalar.activation(m_f[:, t, :], v["b_m", b][:, t, :], ACT.Identity,
-                                         scale=c_m[:, t:t + 1], bias=c0[:, t:t + 1])
-                v["m_f", b] = m_f
-            elif name == "sx":
-                sx = work("sx", b)
-                for t in range(PACK):
-                    nc.vector.scalar_tensor_tensor(sx[:, t, :], v["b_n", b][:, t, :], c_n[:, t:t + 1],
-                                                   v["m_f", b][:, t, :], MULT, ADD)
-                v["sx", b] = sx
-            elif name in ("Fa", "Fg", "Fe"):
-                dst = work("sq_" + name[1], b)
-                nc.scalar.activation(dst[:], v["b_" + name[1], b][:], ACT.Square, scale=1.0,
-                                     bias=0.0 if name == "Fe" else 2.0)
-                v[name[1] + "2", b] = dst
-            elif name == "ak":
-                dst = work("ak", b)
-                for t in range(PACK):
+                dst = fwork("s_f", i)
+                for tt, t in pair:
                     if eng == "s":
-                        nc.scalar.activation(dst[:, t, :], v["a2", b][:, t, :], ACT.Identity,
+                        nc.scalar.activation(dst[:, tt, :], v["b_s", i][:, tt, :], ACT.Identity,
+                                             scale=c_e[:, t:t + 1], bias=c_b[:, t:t + 1])
+                    else:
+                        nc.vector.tensor_scalar(dst[:, tt, :], v["b_s", i][:, tt, :], c_e[:, t:t + 1], c_b[:, t:t + 1], MULT, ADD)
+                v["s_f", i] = dst
+            elif name == "aF":
+                dst = fwork("a_f", i)
+                for tt, t in pair:
+                    nc.vector.tensor_scalar(dst[:, tt, :], v["b_a", i][:, tt, :], c_e[:, t:t + 1], c_b[:, t:t + 1], MULT, ADD)
+                v["a_f", i] = dst
+            elif name == "sG":
+                dst = fwork("s_f", i)
+                for tt, t in pair:
+                    nc.vector.scalar_tensor_tensor(dst[:, tt, :], v["b_g", i][:, tt, :], c_e[:, t:t + 1], v["a_f", i][:, tt, :], MULT, ADD)
+                v["s_f", i] = dst
+            elif name == "X":
+                nc.vector.tensor_tensor(shear_all[:, trange, gcols], v["b_e", i][:], v["s_f", i][:], MULT)
+            elif name == "D":
+                dst = fwork("d", i)
+                nc.vector.tensor_tensor(dst[:], v["b_e", i][:], shear_all[:, trange, gcols], MULT)
+                v["d", i] = dst
+            elif name == "D2":
+                dst = fwork("d", i)
+                nc.vector.tensor_tensor(dst[:], v["fe2", i][:], v["s_f", i][:], MULT)
+                v["d", i] = dst
+            elif name == "mF":
+                dst = fwork("m_f", i)
+                for tt, t in pair:
+                    if vsq.get(blks[0]):
+                        nc.scalar.activation(dst[:, tt, :], v["b_m", i][:, tt, :], ACT.Identity, scale=c_m[:, t:t + 1], bias=c_0[:, t:t + 1])
+                    elif eng == "s":
+                        nc.scalar.activation(dst[:, tt, :], v["b_m", i][:, tt, :], ACT.Copy, scale=c_m[:, t:t + 1])
+                    else:
+                        nc.vector.tensor_scalar(dst[:, tt, :], v["b_m", i][:, tt, :], c_m[:, t:t + 1], 0.0, MULT, ADD)
+                v["m_f", i] = dst
+            elif name == "sx":
+                dst = fwork("sx", i)
+                for tt, t in pair:
+                    nc.vector.scalar_tensor_tensor(dst[:, tt, :], v["b_n", i][:, tt, :], c_n[:, t:t + 1],
+                                                   v["m_f", i][:, tt, :], MULT, ADD)
+                v["sx", i] = dst
+            elif name in ("Fa", "Fg", "Fe"):
+                dst = fwork("fsq_" + name[1], i)
+                nc.scalar.activation(dst[:], v["b_" + name[1], i][:], ACT.Square, scale=1.0,
+                                     bias=0.0 if name == "Fe" else 2.0)
+                v["f" + name[1] + "2", i] = dst
+            elif name == "ak":
+                dst = fwork("ak", i)
+                for tt, t in pair:
+                    if eng == "s":
+                        nc.scalar.activation(dst[:, tt, :], v["fa2", i][:, tt, :], ACT.Identity,
                                              scale=c_n[:, t:t + 1], bias=c_0[:, t:t + 1])
                     else:
-                        two(eng).tensor_scalar(dst[:, t, :], v["a2", b][:, t, :], c_n[:, t:t + 1], c_0[:, t:t + 1], MULT, ADD)
-                v["ak", b] = dst
+                        nc.vector.tensor_scalar(dst[:, tt, :], v["fa2", i][:, tt, :], c_n[:, t:t + 1], c_0[:, t:t + 1], MULT, ADD)
+                v["ak", i] = dst
             elif name == "y":
-                dst = work("y", b)
-                for t in range(PACK):
-                    nc.vector.scalar_tensor_tensor(dst[:, t, :], v["g2", b][:, t, :], c_m[:, t:t + 1],
-                                                   v["ak", b][:, t, :], MULT, ADD)
-                v["y", b] = dst
+                dst = fwork("y", i)
+                for tt, t in pair:
+                    nc.vector.scalar_tensor_tensor(dst[:, tt, :], v["fg2", i][:, tt, :], c_m[:, t:t + 1],
+                                                   v["ak", i][:, tt, :], MULT, ADD)
+                v["y", i] = dst
             elif name == "sy":
-                dst = work("sx", b)
-                for t in range(PACK):
-                    nc.vector.scalar_tensor_tensor(dst[:, t, :], v["e2", b][:, t, :], c_ee[:, t:t + 1],
-                                                   v["y", b][:, t, :], MULT, ADD)
-                v["sx", b] = dst
-            elif name == "D2":
-                d = work("d", b)
-                nc.vector.tensor_tensor(d[:], v["e2", b][:], v["s_f", b][:], MULT)
-                v["d", b] = d
+                dst = fwork("sx", i)
+                for tt, t in pair:
+                    nc.vector.scalar_tensor_tensor(dst[:, tt, :], v["fe2", i][:, tt, :], c_ee[:, t:t + 1],
+                                                   v["y", i][:, tt, :], MULT, ADD)
+                v["sx", i] = dst
             elif name == "AR":
-                ar = work("ar", b)
-                nc.vector.scalar_tensor_tensor(ar[:], v["b_a", b][:], 2.0, v["sx", b][:], ADD, MULT)
-                v["ar", b] = ar
+                dst = fwork("ar", i)
+                nc.vector.scalar_tensor_tensor(dst[:], v["b_a", i][:], 2.0, v["sx", i][:], ADD, MULT)
+                v["ar", i] = dst
             elif name == "P":
-                pxx = work("pxx", b)
-                two(eng).tensor_tensor(pxx[:], v["ar", b][:], v["d", b][:], SUB)
-                v["pxx", b] = pxx
+                dst = fwork("pxx", i)
+                (nc.gpsimd if eng == "g" else nc.vector).tensor_tensor(dst[:], v["ar", i][:], v["d", i][:], SUB)
+                v["pxx", i] = dst
             elif name == "Pc":
-                pc = work("pc", b)
-                two(eng).tensor_tensor(pc[:], v["pxx", b][:], cub[:, :, cols], MULT)
-                v["pc", b] = pc
+                (nc.gpsimd if eng == "g" else nc.vector).tensor_tensor(force[:, trange, gcols], v["pxx", i][:], cub[:, trange, gcols], MULT)
             elif name == "E":
-                eo = work("eo", b)
-                for t in range(PACK):
+                picks = opp_sb[:, blks[0] * LIST_COLS:(blks[-1] + 1) * LIST_COLS]
+                for tt, t in pair:
                     if eng == "s":
-                        nc.scalar.activation(eo[:, t, :], shear[t][:].indirect(picks), ACT.Copy)
+                        nc.scalar.activation(opp_val[:, t, gcols], shear[t].indirect(picks), ACT.Copy)
+                    elif eng == "a":
+                        nc.vector.tensor_tensor(opp_val[:, t, gcols], shear[t].indirect(picks), force[:, t, gcols], ADD)
                     else:
-                        nc.vector.tensor_copy(eo[:, t, :], shear[t][:].indirect(picks))
-                v["eo", b] = eo
-            elif name == "ga":
-                hid = work("hid", b)
-                if ("eo", b) in v:
-                    two(eng).tensor_tensor(hid[:], v["eo", b][:], v["pc", b][:], ADD)
-                else:
-                    for t in range(PACK):
-                        nc.vector.tensor_tensor(hid[:, t, :], shear[t][:].indirect(picks), v["pc", b][:, t, :], ADD)
-                v["hid", b] = hid
+                        nc.vector.tensor_copy(opp_val[:, t, gcols], shear[t].indirect(picks))
+            elif name == "add":
+                part = cols
+                hid = twork("hid", i)
+                nc.vector.tensor_tensor(hid[:], opp_val[:, :, part], force[:, :, part], ADD)
+                v["hid", i] = hid[:]
             elif name == "il":
-                hb = held.tile([P, P, PACK], BF16, name=f"hb{b}", align_bytes=64)
+                part = cols
+                hb = held.tile([P, P, PACK], BF16, name=f"hb{i}", align_bytes=64)
                 dst = hb[:].rearrange("p (c i) t -> p c t i", i=4)
-                src = v["hid", b][:].rearrange("p t (c i) -> p c t i", i=4)
-                if eng == "s":
-                    nc.scalar.copy(dst, src)
+                if eng == "f":
+                    nc.vector.tensor_tensor(dst, opp_val[:, :, part].rearrange("p t (c i) -> p c t i", i=4),
+                                            force[:, :, part].rearrange("p t (c i) -> p c t i", i=4), ADD)
                 else:
-                    nc.vector.tensor_copy(dst, src)
-                v["hb", b] = hb
+                    src = v.get(("hid", i), opp_val[:, :, part]).rearrange("p t (c i) -> p c t i", i=4)
+                    if eng == "s":
+                        nc.scalar.copy(dst, src)
+                    else:
+                        nc.vector.tensor_copy(dst, src)
+                v["hb", i] = hb
             elif name == "q":
-                hw = held.tile([P, P], U32, name=f"hw{b}", align_bytes=64)
-                hs = held.tile([P, P], U8, name=f"hs{b}", align_bytes=64)
-                nc.vector.quantize_mx(hw[:].bitcast(FP8X4), hs[:], v["hb", b][:].rearrange("p c t -> p (c t)"))
-                acc = psum.tile([P, N // P, P], F32, name=f"pre{b % 3}")
-                for h in range(N // P):
-                    nc.tensor.matmul_mx(acc[:, h, :], lhsT=w4w[:, 2 * P * h:2 * P * (h + 1)].bitcast(FP4X4),
-                                        lhsT_scale=w4s[:, 0, P * h:P * (h + 1)],
+                hw = held.tile([P, P], U32, name=f"hw{i}", align_bytes=64)
+                hs = held.tile([P, P], U8, name=f"hs{i}", align_bytes=64)
+                nc.vector.quantize_mx(hw[:].bitcast(FP8X4), hs[:], v["hb", i][:].rearrange("p c t -> p (c t)"))
+                acc = psum.tile([P, N // P, P], F32, name="pre", bufs=3)
+                for m in range(N // P):
+                    nc.tensor.matmul_mx(acc[:, m, :], lhsT=w4w[:, 2 * P * m:2 * P * (m + 1)].bitcast(FP4X4),
+                                        lhsT_scale=w4s[:, 0, P * m:P * (m + 1)],
                                         rhs=hw[:].bitcast(FP8X4), rhs_scale=hs[:], start=True, stop=True)
-                v["acc", b] = acc
+                v["acc", i] = acc
             elif name == "o":
-                res = held.tile([P, N // P, P], F32, name=f"res{b}")
+                res = held.tile([P, N // P, P], F32, name=f"res{i}")
                 if eng == "s":
-                    nc.scalar.copy(res[:], v["acc", b][:])
+                    nc.scalar.copy(res[:], v["acc", i][:])
                 else:
-                    nc.vector.tensor_copy(res[:], v["acc", b][:])
+                    nc.vector.tensor_copy(res[:], v["acc", i][:])
                 nc.sync.dma_start(out=out_v[:, :, cols], in_=res[:])
 
-        for word in "G.0.v Ma.0.p Mg.0.p Me.0.p G.1.v Ta.0.s Tg.0.s Te.0.s Hs.0.p He.0.p Ha.0.p Hg.0.p Ma.1.p Mg.1.p Me.1.p G.2.v G.3.v sF.0.s Fe.0.s X.0.v D2.0.v Ta.1.s Tg.1.s Te.1.s Hs.1.p He.1.p Ma.2.p Mg.2.p Me.2.p Fa.0.s ak.0.v Fg.0.s y.0.v sy.0.v AR.0.v Ha.1.p Hg.1.p sF.1.s Fe.1.s X.1.v D2.1.v P.0.v Pc.0.v Ta.2.s Tg.2.s Te.2.s Hs.2.p He.2.p Ma.3.p Mg.3.p Me.3.p Fa.1.s ak.1.v Fg.1.s y.1.v sy.1.v AR.1.v Ha.2.p Hg.2.p sF.2.s Fe.2.s X.2.v D2.2.v P.1.v Pc.1.v Ta.3.s Tg.3.s Te.3.s Hs.3.p He.3.p Fa.2.s ak.2.s Fg.2.s y.2.v sy.2.v AR.2.v Ha.3.p Hg.3.p sF.3.s Fe.3.s X.3.v D2.3.v P.2.v Pc.2.v ga.0.v il.0.s q.0.v o.0.s Fa.3.s ak.3.s Fg.3.s y.3.v sy.3.v AR.3.v E.3.s E.1.s ga.1.v il.1.s q.1.v o.1.s P.3.v Pc.3.v E.2.s ga.2.v il.2.s q.2.v o.2.s ga.3.v il.3.v q.3.v o.3.s".split():
-            name, b, eng = word.split(".")
-            step(name, int(b), eng)
+        for word in "Gs.0.v Gs.1.v G.0.v G.1.v G.2.v G.3.v Ma.0.v Ta.0.s Mg.0.v Tg.0.s Me.0.v Te.0.s Hs.0.p He.0.p Ha.0.p Hg.0.p Fe.0.s sF.0.v X.0.v D2.0.v Ma.1.v Ta.1.s Mg.1.v Tg.1.s Me.1.v Te.1.s Hs.1.p He.1.p Fa.0.s ak.0.v Fg.0.s y.0.v sy.0.v AR.0.v Ha.1.p Hg.1.p Fe.1.s sF.1.v X.1.v D2.1.v P.0.v Pc.0.v Ma.2.v Ta.2.s Mg.2.v Tg.2.s Me.2.v Te.2.s Hs.2.p He.2.p Fa.1.s ak.1.v Fg.1.s y.1.v sy.1.v AR.1.v Qe.2.s Qg.2.s Qa.2.s Hm.2.p Hn.2.p Ha.2.p sF.2.s X.2.v D.2.v P.1.v Pc.1.v Ma.3.v Ta.3.s Mg.3.v Tg.3.s Me.3.v Te.3.s Hs.3.p He.3.p sF.3.s X.3.v D.3.v mF.2.s sx.2.v AR.2.v Qe.3.s Qg.3.s Qa.3.s Hm.3.p Hn.3.p Ha.3.p P.2.v Pc.2.v mF.3.s sx.3.v AR.3.v E.0.s il.0.f q.0.v o.0.s E.1.s il.1.f q.1.v o.1.s E.2.s P.3.v Pc.3.v E.3.s il.2.f q.2.v o.2.s il.3.f q.3.v o.3.s".split():
+            name, i, eng = word.split(".")
+            step(name, int(i), eng)

@@ -46,7 +46,10 @@ def tile_picked_ystvkf_shear_p_kernel(
         xs_all = held.tile([P, PASSES, T], U8, name="xs_all", align_bytes=64)
         xw_all = held.tile([P, PASSES, T], U32, name="xw_all", align_bytes=64)
         ww = [held.tile([P, PASSES, 2 * H], U8, name=f"ww{i}", align_bytes=64) for i in range(3)]
-        ws = [held.tile([P, PASSES, H], U8, name=f"ws{i}", align_bytes=64) for i in range(3)]
+        ws_first = held.tile([P, PASSES, H], U8, name="ws0", align_bytes=64)
+        ws_stage = held.tile([P, 2, PASSES, 4, H], U8, name="ws_stage", align_bytes=64)
+        ws_rest = held.tile([P, 2, PASSES, H], U8, name="ws_rest", align_bytes=64)
+        ws = [ws_first[:], ws_rest[:, 0], ws_rest[:, 1]]
         w4w = held.tile([P, 2 * N], U8, name="w4w", align_bytes=64)
         w4s = held.tile([P, 1, N], U8, name="w4s", align_bytes=64)
         lam = held.tile([P, PACK], F32, name="lam")
@@ -59,8 +62,8 @@ def tile_picked_ystvkf_shear_p_kernel(
         ORD = "age"
 
         nc.gpsimd.memset(xs_all[:].bitcast(I32), 0)
-        for i in range(3):
-            nc.vector.memset(ws[i][:].bitcast(I32), 0)
+        nc.vector.memset(ws_rest[:].bitcast(I32), 0)
+        nc.vector.memset(ws_first[:].bitcast(I32), 0)
         nc.vector.memset(w4s[:].bitcast(I32), 0)
 
         def load_words(i):
@@ -70,17 +73,19 @@ def tile_picked_ystvkf_shear_p_kernel(
             nc.sync.dma_start(out=xw_all[:].bitcast(I32),
                               in_=x_words.rearrange("o p c r -> p o (c r)").bitcast(I32))
 
+        nc.gpsimd.dma_start(out=uni[:], in_=unit.rearrange("(p t) o -> p (t o)", t=PACK))
+        nc.gpsimd.dma_start(out=lam[:], in_=lame.rearrange("(p t) o -> p (t o)", t=PACK))
         nc.sync.dma_start(offs_sb[:], offs)
+        nc.sync.dma_start(out=ws_stage[:].bitcast(I32)[0:P:32, 0], in_=w_scales[1].bitcast(I32).rearrange("o (q r) c -> q o r c", r=4))
+        nc.sync.dma_start(out=ws_stage[:].bitcast(I32)[0:P:32, 1], in_=w_scales[2].bitcast(I32).rearrange("o (q r) c -> q o r c", r=4))
         load_scale_rows(nc.sync, xs_all[:], x_scales)
-        nc.sync.dma_start(out=uni[:], in_=unit.rearrange("(p t) o -> p (t o)", t=PACK))
-        nc.sync.dma_start(out=lam[:], in_=lame.rearrange("(p t) o -> p (t o)", t=PACK))
         load_x(0)
         load_scale_rows(nc.sync, ws[0][:], w_scales[0])
         load_words(0)
         load_words(1)
         load_words(2)
-        load_scale_rows(nc.sync, ws[1][:], w_scales[1])
-        load_scale_rows(nc.gpsimd, ws[2][:], w_scales[2])
+        for r in range(4):
+            nc.sync.dma_start(out=ws_rest[:].bitcast(I32)[r:P:32], in_=ws_stage[:].bitcast(I32)[0:P:32, :, :, r, :])
         nc.sync.dma_start(out=cub[:], in_=cubw.rearrange("(p t) j -> p t j", t=PACK))
         nc.sync.dma_start(opp_sb[:], opp)
         nc.sync.dma_start(out=w4w[:].bitcast(I32), in_=w4_words[0].bitcast(I32))
@@ -255,6 +260,10 @@ def tile_picked_ystvkf_shear_p_kernel(
                         nc.vector.tensor_tensor(opp_val[:, t, gcols], shear[t].indirect(picks), force[:, t, gcols], ADD)
                     else:
                         nc.vector.tensor_copy(opp_val[:, t, gcols], shear[t].indirect(picks))
+            elif name == "E2":
+                picks = opp_sb[:, i * 16:(i + 1) * 16]
+                for t in range(PACK):
+                    nc.scalar.activation(opp_val[:, t, i * W:(i + 1) * W], shear[t].indirect(picks), ACT.Copy)
             elif name == "add":
                 part = cols
                 hid = twork("hid", i)
@@ -292,6 +301,6 @@ def tile_picked_ystvkf_shear_p_kernel(
                     nc.vector.tensor_copy(res[:], v["acc", i][:])
                 nc.sync.dma_start(out=out_v[:, :, cols], in_=res[:])
 
-        for word in "Gs.0.v Gs.1.v G.0.v G.1.v G.2.v G.3.v Ma.0.v Ta.0.s Mg.0.v Tg.0.s Me.0.v Te.0.s Hs.0.p He.0.p Ha.0.p Hg.0.p Fe.0.s sF.0.v X.0.v D2.0.v Ma.1.v Ta.1.s Mg.1.v Tg.1.s Me.1.v Te.1.s Hs.1.p He.1.p Fa.0.s ak.0.v Fg.0.s y.0.v sy.0.v AR.0.v Ha.1.p Hg.1.p Fe.1.s sF.1.v X.1.v D2.1.v P.0.v Pc.0.v Ma.2.v Ta.2.s Mg.2.v Tg.2.s Me.2.v Te.2.s Hs.2.p He.2.p Fa.1.s ak.1.v Fg.1.s y.1.v sy.1.v AR.1.v Qe.2.s Qg.2.s Qa.2.s Hm.2.p Hn.2.p Ha.2.p sF.2.s X.2.v D.2.v P.1.v Pc.1.v Ma.3.v Ta.3.s Mg.3.v Tg.3.s Me.3.v Te.3.s Hs.3.p He.3.p sF.3.s X.3.v D.3.v mF.2.s sx.2.v AR.2.v Qe.3.s Qg.3.s Qa.3.s Hm.3.p Hn.3.p Ha.3.p P.2.v Pc.2.v mF.3.s sx.3.v AR.3.v E.0.s il.0.f q.0.v o.0.s E.1.s il.1.f q.1.v o.1.s E.2.s P.3.v Pc.3.v E.3.s il.2.f q.2.v o.2.s il.3.f q.3.v o.3.s".split():
+        for word in "Gs.0.v Gs.1.v G.0.v G.1.v G.2.v G.3.v Ma.0.v Ta.0.s Mg.0.v Tg.0.s Me.0.v Te.0.s Hs.0.p He.0.p Ha.0.p Hg.0.p Fe.0.s sF.0.v X.0.v D2.0.v Ma.1.v Ta.1.s Mg.1.v Tg.1.s Me.1.v Te.1.s Hs.1.p He.1.p Fa.0.s ak.0.v Fg.0.s y.0.v sy.0.v AR.0.v Ha.1.p Hg.1.p Fe.1.s sF.1.v X.1.v D2.1.v P.0.v Pc.0.v Ma.2.v Ta.2.s Mg.2.v Tg.2.s Me.2.v Te.2.s Hs.2.p He.2.p Fa.1.s ak.1.v Fg.1.s y.1.v sy.1.v AR.1.v Ha.2.p Hg.2.p Fe.2.s sF.2.s X.2.v D2.2.v P.1.v Pc.1.v Ma.3.v Ta.3.s Mg.3.v Tg.3.s Me.3.v Te.3.s Hs.3.p He.3.p Fe.3.s sF.3.s X.3.v D2.3.v Fa.2.s ak.2.s Fg.2.s y.2.v sy.2.v AR.2.v Ha.3.p Hg.3.p P.2.v Pc.2.v Fa.3.s ak.3.s Fg.3.s y.3.v sy.3.v AR.3.v E2.0.s il.0.f q.0.v o.0.s il.1.f q.1.v o.1.s E2.1.s P.3.v Pc.3.v il.2.f q.2.v o.2.s il.3.f q.3.v o.3.s".split():
             name, i, eng = word.split(".")
             step(name, int(i), eng)

@@ -77,8 +77,9 @@ def tile_picked_ystvkf_shear_p_kernel(
         nc.gpsimd.dma_start(out=lam[:], in_=lame.rearrange("(p t) o -> p (t o)", t=PACK))
         nc.sync.dma_start(offs_sb[:], offs)
         nc.sync.dma_start(out=ws_stage[:].bitcast(I32)[0:P:32, 0], in_=w_scales[1].bitcast(I32).rearrange("o (q r) c -> q o r c", r=4))
-        nc.sync.dma_start(out=ws_stage[:].bitcast(I32)[0:P:32, 1], in_=w_scales[2].bitcast(I32).rearrange("o (q r) c -> q o r c", r=4))
-        load_scale_rows(nc.sync, xs_all[:], x_scales)
+        nc.scalar.dma_start(out=ws_stage[:].bitcast(I32)[0:P:32, 1], in_=w_scales[2].bitcast(I32).rearrange("o (q r) c -> q o r c", r=4))
+        load_scale_rows(nc.sync, xs_all[:], x_scales, (0, 1,))
+        load_scale_rows(nc.scalar, xs_all[:], x_scales, (2, 3,))
         load_x(0)
         load_scale_rows(nc.sync, ws[0][:], w_scales[0])
         load_words(0)
@@ -266,7 +267,7 @@ def tile_picked_ystvkf_shear_p_kernel(
                     nc.scalar.activation(opp_val[:, t, i * W:(i + 1) * W], shear[t].indirect(picks), ACT.Copy)
             elif name == "add":
                 part = cols
-                hid = twork("hid", i)
+                hid = held.tile([P, PACK, P], BF16, name=f"hid{i}")
                 nc.vector.tensor_tensor(hid[:], opp_val[:, :, part], force[:, :, part], ADD)
                 v["hid", i] = hid[:]
             elif name == "il":
@@ -277,7 +278,8 @@ def tile_picked_ystvkf_shear_p_kernel(
                     nc.vector.tensor_tensor(dst, opp_val[:, :, part].rearrange("p t (c i) -> p c t i", i=4),
                                             force[:, :, part].rearrange("p t (c i) -> p c t i", i=4), ADD)
                 else:
-                    src = v.get(("hid", i), opp_val[:, :, part]).rearrange("p t (c i) -> p c t i", i=4)
+                    dst = hb[:]
+                    src = v["hid", i].rearrange("p t c -> p c t")
                     if eng == "s":
                         nc.scalar.copy(dst, src)
                     else:
@@ -301,6 +303,6 @@ def tile_picked_ystvkf_shear_p_kernel(
                     nc.vector.tensor_copy(res[:], v["acc", i][:])
                 nc.sync.dma_start(out=out_v[:, :, cols], in_=res[:])
 
-        for word in "Gs.0.v Gs.1.v G.0.v G.1.v G.2.v G.3.v Ma.0.v Ta.0.s Mg.0.v Tg.0.s Me.0.v Te.0.s Hs.0.p He.0.p Ha.0.p Hg.0.p Fe.0.s sF.0.v X.0.v D2.0.v Ma.1.v Ta.1.s Mg.1.v Tg.1.s Me.1.v Te.1.s Hs.1.p He.1.p Fa.0.s ak.0.v Fg.0.s y.0.v sy.0.v AR.0.v Ha.1.p Hg.1.p Fe.1.s sF.1.v X.1.v D2.1.v P.0.v Pc.0.v Ma.2.v Ta.2.s Mg.2.v Tg.2.s Me.2.v Te.2.s Hs.2.p He.2.p Fa.1.s ak.1.v Fg.1.s y.1.v sy.1.v AR.1.v Ha.2.p Hg.2.p Fe.2.s sF.2.s X.2.v D2.2.v P.1.v Pc.1.v Ma.3.v Ta.3.s Mg.3.v Tg.3.s Me.3.v Te.3.s Hs.3.p He.3.p Fe.3.s sF.3.s X.3.v D2.3.v Fa.2.s ak.2.s Fg.2.s y.2.v sy.2.v AR.2.v Ha.3.p Hg.3.p P.2.v Pc.2.v Fa.3.s ak.3.s Fg.3.s y.3.v sy.3.v AR.3.v E2.0.s il.0.f q.0.v o.0.s il.1.f q.1.v o.1.s E2.1.s P.3.v Pc.3.v il.2.f q.2.v o.2.s il.3.f q.3.v o.3.s".split():
+        for word in "Gs.0.v Gs.1.v G.0.v G.1.v G.2.v G.3.v Ma.0.v Ta.0.s Ma.1.v Ta.1.s Mg.0.v Tg.0.s Me.0.v Te.0.s Ha.0.v Hs.0.v Hg.0.v He.0.v Fa.0.s sF.0.v X.0.v ak.0.v Fg.0.s Fe.0.s Mg.1.v Tg.1.s Me.1.v Te.1.s Ha.1.v Hs.1.v Hg.1.v He.1.v Fa.1.s sF.1.v X.1.v ak.1.s Fg.1.s Fe.1.s y.0.v D2.0.v sy.0.v AR.0.v P.0.v Pc.0.v Ma.2.v Ta.2.s Mg.2.v Tg.2.s Me.2.v Te.2.s Ha.2.v Hs.2.v Hg.2.v He.2.v Fa.2.s sF.2.s X.2.v ak.2.s Fg.2.s Fe.2.s y.1.v D2.1.v sy.1.v AR.1.v P.1.v Pc.1.v Ma.3.v Ta.3.s Mg.3.v Tg.3.s Me.3.v Te.3.s Ha.3.v Hs.3.v Hg.3.v He.3.v Fa.3.s sF.3.s X.3.v ak.3.s Fg.3.s Fe.3.s y.2.v D2.2.v sy.2.v AR.2.v P.2.v Pc.2.v y.3.v D2.3.v sy.3.v AR.3.v P.3.v Pc.3.v E.0.s add.0.v il.0.v q.0.v o.0.s E.1.s add.1.v il.1.v q.1.v o.1.s E.2.s add.2.v il.2.v q.2.v o.2.s E.3.s add.3.v il.3.v q.3.v o.3.s".split():
             name, i, eng = word.split(".")
             step(name, int(i), eng)

from contextlib import ExitStack

import concourse.mybir as mybir
from concourse.masks import make_identity

K, T, S, N, H = 1024, 1024, 512, 256, 512
FLOPS = 2 * (3 * K * H * S + H * N * S)

F32 = mybir.dt.float32
BF16 = mybir.dt.bfloat16
I32 = mybir.dt.int32
U32 = mybir.dt.uint32
U16 = mybir.dt.uint16
U8 = mybir.dt.uint8
FP8X4 = mybir.dt.float8_e4m3fn_x4
FP4X4 = mybir.dt.float4_e2m1fn_x4
ACT = mybir.ActivationFunctionType
ADD = mybir.AluOpType.add
SUB = mybir.AluOpType.subtract
MULT = mybir.AluOpType.mult

P = 128
PACK = 4
PASSES = K // (P * PACK)
BLOCKS = S // P
LIST_COLS = P // 16


def load_scale_rows(queue, plane, scales, which=range(4)):
    rows = scales.bitcast(I32).rearrange("o (q r) c -> r q o c", r=4)
    for r in which:
        queue.dma_start(out=plane.bitcast(I32)[r:P:32, :, :], in_=rows[r])


def tile_picked_ystvkf_shear_p_kernel(
    tc, x_words, x_scales, w1_words, w1_scales, w2_words, w2_scales, w3_words, w3_scales,
    lame, cubw, unit, w4_words, w4_scales, offs, opp, out,
):
    nc = tc.nc
    with ExitStack() as ctx:
        held = ctx.enter_context(tc.tile_pool(name="held", bufs=1))
        psum = ctx.enter_context(tc.psum_pool(name="psum", bufs=1))

        offs_sb = held.tile([P, S // 16], U16, name="offs_sb")
        opp_sb = held.tile([P, S // 16], U16, name="opp_sb")
        xs_all = held.tile([P, PASSES, T], U8, name="xs_all", align_bytes=64)
        xw_all = held.tile([P, PASSES, T], U32, name="xw_all", align_bytes=64)
        ww = [held.tile([P, PASSES, 2 * H], U8, name=f"ww{i}", align_bytes=64) for i in range(3)]
        ws_first = held.tile([P, PASSES, H], U8, name="ws0", align_bytes=64)
        ws_stage = held.tile([P, 2, PASSES, 4, H], U8, name="ws_stage", align_bytes=64)
        ws_rest = held.tile([P, 2, PASSES, H], U8, name="ws_rest", align_bytes=64)
        ws = [ws_first[:], ws_rest[:, 0], ws_rest[:, 1]]
        w4w = held.tile([P, 2 * N], U8, name="w4w", align_bytes=64)
        w4s = held.tile([P, 1, N], U8, name="w4s", align_bytes=64)
        lam = held.tile([P, PACK], F32, name="lam")
        uni = held.tile([P, PACK], F32, name="uni")
        cub = held.tile([P, PACK, S], F32, name="cub")
        ident = held.tile([P, P], F32, name="ident")

        w_words = (w1_words, w3_words, w2_words)
        w_scales = (w1_scales, w3_scales, w2_scales)
        ORD = "age"

        nc.gpsimd.memset(xs_all[:].bitcast(I32), 0)
        nc.vector.memset(ws_rest[:].bitcast(I32), 0)
        nc.vector.memset(ws_first[:].bitcast(I32), 0)
        nc.vector.memset(w4s[:].bitcast(I32), 0)

        def load_words(i):
            nc.sync.dma_start(out=ww[i][:].bitcast(I32), in_=w_words[i].bitcast(I32).rearrange("o p c -> p o c"))

        def load_x(o):
            nc.sync.dma_start(out=xw_all[:].bitcast(I32),
                              in_=x_words.rearrange("o p c r -> p o (c r)").bitcast(I32))

        nc.gpsimd.dma_start(out=uni[:], in_=unit.rearrange("(p t) o -> p (t o)", t=PACK))
        nc.gpsimd.dma_start(out=lam[:], in_=lame.rearrange("(p t) o -> p (t o)", t=PACK))
        nc.sync.dma_start(offs_sb[:], offs)
        nc.sync.dma_start(out=ws_stage[:].bitcast(I32)[0:P:32, 0], in_=w_scales[1].bitcast(I32).rearrange("o (q r) c -> q o r c", r=4))
        nc.scalar.dma_start(out=ws_stage[:].bitcast(I32)[0:P:32, 1], in_=w_scales[2].bitcast(I32).rearrange("o (q r) c -> q o r c", r=4))
        load_scale_rows(nc.sync, xs_all[:], x_scales, (0, 1,))
        load_scale_rows(nc.scalar, xs_all[:], x_scales, (2, 3,))
        load_x(0)
        load_scale_rows(nc.sync, ws[0][:], w_scales[0])
        load_words(0)
        load_words(1)
        load_words(2)
        for r in range(4):
            nc.sync.dma_start(out=ws_rest[:].bitcast(I32)[r:P:32], in_=ws_stage[:].bitcast(I32)[0:P:32, :, :, r, :])
        nc.sync.dma_start(out=cub[:], in_=cubw.rearrange("(p t) j -> p t j", t=PACK))
        nc.sync.dma_start(opp_sb[:], opp)
        nc.sync.dma_start(out=w4w[:].bitcast(I32), in_=w4_words[0].bitcast(I32))
        load_scale_rows(nc.sync, w4s[:], w4_scales)
        make_identity(nc, ident[:])

        ce = nc.gpsimd
        LINES = ((0.0, -0.125), (0.0, -0.5), (0.0625, 0.0), (0.0625, 0.125), (0.125, 0.125), (-0.5, -0.5))
        lin = held.tile([P, len(LINES), PACK], F32, name="lin")
        coef = held.tile([P, len(LINES), PACK], F32, name="coef")
        for n, (slope, offset) in enumerate(LINES):
            if slope == 0.0:
                ce.memset(lin[:, n, :], offset)
            else:
                ce.tensor_scalar(lin[:, n, :], lam[:], slope, offset, MULT, ADD)
        ce.tensor_tensor(coef[:], lin[:], uni[:].unsqueeze(1).to_broadcast([P, len(LINES), PACK]), MULT)
        c_e, c_b, c_m, c_n, c_ee, c_0 = (coef[:, n, :] for n in range(len(LINES)))

        xs = [held.tile([P, S], U8, name=f"xs{o}", align_bytes=64) for o in range(PASSES)]
        xw = {}
        shear_all = held.tile([P, PACK, S], F32, name="shear")
        shear = [shear_all[:, t, :] for t in range(PACK)]
        out_v = out.rearrange("(h p) j -> p h j", p=P)
        W = 2 * P
        v = {}
        vsq = {}
        force = held.tile([P, PACK, S], F32, name="force")
        opp_val = held.tile([P, PACK, S], F32, name="eo")
        UNITS = [[[0],[0,1,2,3]],[[1],[0,1,2,3]],[[2],[0,1,2,3]],[[3],[0,1,2,3]]]

        def twork(name, b):
            return held.tile([P, PACK, P], F32, name=f"{name}{b}")

        def fwork(name, u):
            return held.tile([P, len(UNITS[u][1]), P * len(UNITS[u][0])], F32, name=f"{name}{u}")

        def step(name, i, eng):
            blks, ts = UNITS[i]
            gcols = slice(blks[0] * P, (blks[-1] + 1) * P)
            pair = list(enumerate(ts))
            trange = slice(ts[0], ts[-1] + 1)
            cols = slice(i * P, (i + 1) * P)
            if name == "Gs":
                n = S // 2
                for o in range(PASSES):
                    nc.vector.tensor_copy(xs[o][:, i * n:(i + 1) * n], xs_all[:, o, :].indirect(offs_sb[:, i * n // 16:(i + 1) * n // 16]))
            elif name == "G":
                for o in range(PASSES):
                    xw[o, i] = held.tile([P, P], U32, name=f"xw{o}", bufs=4, align_bytes=64)
                    nc.vector.tensor_copy(xw[o, i][:], xw_all[:, o, :].indirect(offs_sb[:, i * LIST_COLS:(i + 1) * LIST_COLS]))
            elif name in ("Ma", "Mg", "Me"):
                k = ORD.index(name[1])
                pre = psum.tile([P, H], F32, name="pre", bufs=3)
                for o in range(PASSES):
                    nc.tensor.matmul_mx(pre[:], lhsT=xw[o, i][:].bitcast(FP8X4), lhsT_scale=xs[o][:, cols],
                                        rhs=ww[k][:, o, :].bitcast(FP4X4), rhs_scale=ws[k][:, o, :],
                                        start=(o == 0), stop=(o == PASSES - 1))
                v["pre" + name[1], i] = pre
            elif name in ("Ta", "Tg", "Te"):
                y = twork("th_" + name[1], i)
                nc.scalar.activation(y[:], v["pre" + name[1], i][:].rearrange("p (m t) -> p t m", t=PACK), ACT.Tanh)
                v[name[1], i] = y
            elif name in ("Qa", "Qg", "Qe"):
                src = v[name[1], i]
                dst = twork("sq_" + name[1], i)
                if name == "Qe" and eng == "s":
                    nc.scalar.activation(dst[:], src[:], ACT.Square)
                elif name == "Qe":
                    nc.vector.tensor_tensor(dst[:], src[:], src[:], MULT)
                elif eng == "s":
                    nc.scalar.activation(dst[:], src[:], ACT.Square, scale=1.0, bias=2.0)
                    vsq[i] = True
                else:
                    nc.vector.scalar_tensor_tensor(dst[:], src[:], 4.0, src[:], ADD, MULT)
                v[name[1] + "2", i] = dst
            elif name[0] == "H":
                terms = {"s": ("a", "g"), "e": ("e",), "m": ("e2", "g2"), "n": ("e2", "a2"), "a": ("a",), "g": ("g",)}[name[1]]
                tag = {"m": "g", "n": "a"}.get(name[1], name[1])
                bank = psum.tile([P, len(ts), P * len(blks)], F32, name="b_" + tag, bufs={"a":2,"e":1,"g":1,"s":1}[tag])
                moves = [(x, bb, tt, t) for bb in range(len(blks)) for x in terms for tt, t in pair]
                for n, (x, bb, tt, t) in enumerate(moves):
                    nc.tensor.matmul(bank[:, tt, bb * P:(bb + 1) * P], v[x, blks[bb]][:, t, :], ident[:],
                                     is_transpose=True, start=(n == 0), stop=(n == len(moves) - 1))
                v["b_" + name[1], i] = bank
            elif name == "sF":
                dst = fwork("s_f", i)
                for tt, t in pair:
                    if eng == "s":
                        nc.scalar.activation(dst[:, tt, :], v["b_s", i][:, tt, :], ACT.Identity,
                                             scale=c_e[:, t:t + 1], bias=c_b[:, t:t + 1])
                    else:
                        nc.vector.tensor_scalar(dst[:, tt, :], v["b_s", i][:, tt, :], c_e[:, t:t + 1], c_b[:, t:t + 1], MULT, ADD)
                v["s_f", i] = dst
            elif name == "aF":
                dst = fwork("a_f", i)
                for tt, t in pair:
                    nc.vector.tensor_scalar(dst[:, tt, :], v["b_a", i][:, tt, :], c_e[:, t:t + 1], c_b[:, t:t + 1], MULT, ADD)
                v["a_f", i] = dst
            elif name == "sG":
                dst = fwork("s_f", i)
                for tt, t in pair:
                    nc.vector.scalar_tensor_tensor(dst[:, tt, :], v["b_g", i][:, tt, :], c_e[:, t:t + 1], v["a_f", i][:, tt, :], MULT, ADD)
                v["s_f", i] = dst
            elif name == "X":
                nc.vector.tensor_tensor(shear_all[:, trange, gcols], v["b_e", i][:], v["s_f", i][:], MULT)
            elif name == "D":
                dst = fwork("d", i)
                nc.vector.tensor_tensor(dst[:], v["b_e", i][:], shear_all[:, trange, gcols], MULT)
                v["d", i] = dst
            elif name == "D2":
                dst = fwork("d", i)
                nc.vector.tensor_tensor(dst[:], v["fe2", i][:], v["s_f", i][:], MULT)
                v["d", i] = dst
            elif name == "mF":
                dst = fwork("m_f", i)
                for tt, t in pair:
                    if vsq.get(blks[0]):
                        nc.scalar.activation(dst[:, tt, :], v["b_m", i][:, tt, :], ACT.Identity, scale=c_m[:, t:t + 1], bias=c_0[:, t:t + 1])
                    elif eng == "s":
                        nc.scalar.activation(dst[:, tt, :], v["b_m", i][:, tt, :], ACT.Copy, scale=c_m[:, t:t + 1])
                    else:
                        nc.vector.tensor_scalar(dst[:, tt, :], v["b_m", i][:, tt, :], c_m[:, t:t + 1], 0.0, MULT, ADD)
                v["m_f", i] = dst
            elif name == "sx":
                dst = fwork("sx", i)
                for tt, t in pair:
                    nc.vector.scalar_tensor_tensor(dst[:, tt, :], v["b_n", i][:, tt, :], c_n[:, t:t + 1],
                                                   v["m_f", i][:, tt, :], MULT, ADD)
                v["sx", i] = dst
            elif name in ("Fa", "Fg", "Fe"):
                dst = fwork("fsq_" + name[1], i)
                nc.scalar.activation(dst[:], v["b_" + name[1], i][:], ACT.Square, scale=1.0,
                                     bias=0.0 if name == "Fe" else 2.0)
                v["f" + name[1] + "2", i] = dst
            elif name == "ak":
                dst = fwork("ak", i)
                for tt, t in pair:
                    if eng == "s":
                        nc.scalar.activation(dst[:, tt, :], v["fa2", i][:, tt, :], ACT.Identity,
                                             scale=c_n[:, t:t + 1], bias=c_0[:, t:t + 1])
                    else:
                        nc.vector.tensor_scalar(dst[:, tt, :], v["fa2", i][:, tt, :], c_n[:, t:t + 1], c_0[:, t:t + 1], MULT, ADD)
                v["ak", i] = dst
            elif name == "y":
                dst = fwork("y", i)
                for tt, t in pair:
                    nc.vector.scalar_tensor_tensor(dst[:, tt, :], v["fg2", i][:, tt, :], c_m[:, t:t + 1],
                                                   v["ak", i][:, tt, :], MULT, ADD)
                v["y", i] = dst
            elif name == "sy":
                dst = fwork("sx", i)
                for tt, t in pair:
                    nc.vector.scalar_tensor_tensor(dst[:, tt, :], v["fe2", i][:, tt, :], c_ee[:, t:t + 1],
                                                   v["y", i][:, tt, :], MULT, ADD)
                v["sx", i] = dst
            elif name == "AR":
                dst = fwork("ar", i)
                nc.vector.scalar_tensor_tensor(dst[:], v["b_a", i][:], 2.0, v["sx", i][:], ADD, MULT)
                v["ar", i] = dst
            elif name == "P":
                dst = fwork("pxx", i)
                (nc.gpsimd if eng == "g" else nc.vector).tensor_tensor(dst[:], v["ar", i][:], v["d", i][:], SUB)
                v["pxx", i] = dst
            elif name == "Pc":
                (nc.gpsimd if eng == "g" else nc.vector).tensor_tensor(force[:, trange, gcols], v["pxx", i][:], cub[:, trange, gcols], MULT)
            elif name == "E":
                picks = opp_sb[:, blks[0] * LIST_COLS:(blks[-1] + 1) * LIST_COLS]
                for tt, t in pair:
                    if eng == "s":
                        nc.scalar.activation(opp_val[:, t, gcols], shear[t].indirect(picks), ACT.Copy)
                    elif eng == "a":
                        nc.vector.tensor_tensor(opp_val[:, t, gcols], shear[t].indirect(picks), force[:, t, gcols], ADD)
                    else:
                        nc.vector.tensor_copy(opp_val[:, t, gcols], shear[t].indirect(picks))
            elif name == "E2":
                picks = opp_sb[:, i * 16:(i + 1) * 16]
                for t in range(PACK):
                    nc.scalar.activation(opp_val[:, t, i * W:(i + 1) * W], shear[t].indirect(picks), ACT.Copy)
            elif name == "add":
                part = cols
                hid = held.tile([P, PACK, P], BF16, name=f"hid{i}")
                nc.vector.tensor_tensor(hid[:], opp_val[:, :, part], force[:, :, part], ADD)
                v["hid", i] = hid[:]
            elif name == "il":
                part = cols
                hb = held.tile([P, P, PACK], BF16, name=f"hb{i}", align_bytes=64)
                dst = hb[:].rearrange("p (c i) t -> p c t i", i=4)
                if eng == "f":
                    nc.vector.tensor_tensor(dst, opp_val[:, :, part].rearrange("p t (c i) -> p c t i", i=4),
                                            force[:, :, part].rearrange("p t (c i) -> p c t i", i=4), ADD)
                else:
                    dst = hb[:]
                    src = v["hid", i].rearrange("p t c -> p c t")
                    if eng == "s":
                        nc.scalar.copy(dst, src)
                    else:
                        nc.vector.tensor_copy(dst, src)
                v["hb", i] = hb
            elif name == "q":
                hw = held.tile([P, P], U32, name=f"hw{i}", align_bytes=64)
                hs = held.tile([P, P], U8, name=f"hs{i}", align_bytes=64)
                nc.vector.quantize_mx(hw[:].bitcast(FP8X4), hs[:], v["hb", i][:].rearrange("p c t -> p (c t)"))
                acc = psum.tile([P, N // P, P], F32, name="pre", bufs=3)
                for m in range(N // P):
                    nc.tensor.matmul_mx(acc[:, m, :], lhsT=w4w[:, 2 * P * m:2 * P * (m + 1)].bitcast(FP4X4),
                                        lhsT_scale=w4s[:, 0, P * m:P * (m + 1)],
                                        rhs=hw[:].bitcast(FP8X4), rhs_scale=hs[:], start=True, stop=True)
                v["acc", i] = acc
            elif name == "o":
                res = held.tile([P, N // P, P], F32, name=f"res{i}")
                if eng == "s":
                    nc.scalar.copy(res[:], v["acc", i][:])
                else:
                    nc.vector.tensor_copy(res[:], v["acc", i][:])
                nc.sync.dma_start(out=out_v[:, :, cols], in_=res[:])

        for word in "Gs.0.v Gs.1.v G.0.v G.1.v G.2.v G.3.v Ma.0.v Ta.0.s Ma.1.v Ta.1.s Mg.0.v Tg.0.s Me.0.v Te.0.s Ha.0.v Hs.0.v Hg.0.v He.0.v Fa.0.s sF.0.v X.0.v ak.0.v Fg.0.s Fe.0.s Mg.1.v Tg.1.s Me.1.v Te.1.s Ha.1.v Hs.1.v Hg.1.v He.1.v Fa.1.s sF.1.v X.1.v ak.1.s Fg.1.s Fe.1.s y.0.v D2.0.v sy.0.v AR.0.v P.0.v Pc.0.v Ma.2.v Ta.2.s Mg.2.v Tg.2.s Me.2.v Te.2.s Ha.2.v Hs.2.v Hg.2.v He.2.v Fa.2.s sF.2.s X.2.v ak.2.s Fg.2.s Fe.2.s y.1.v D2.1.v sy.1.v AR.1.v P.1.v Pc.1.v Ma.3.v Ta.3.s Mg.3.v Tg.3.s Me.3.v Te.3.s Ha.3.v Hs.3.v Hg.3.v He.3.v Fa.3.s sF.3.s X.3.v ak.3.s Fg.3.s Fe.3.s y.2.v D2.2.v sy.2.v AR.2.v P.2.v Pc.2.v y.3.v D2.3.v sy.3.v AR.3.v P.3.v Pc.3.v E.0.s add.0.v il.0.v q.0.v o.0.s E.1.s add.1.v il.1.v q.1.v o.1.s E.2.s add.2.v il.2.v q.2.v o.2.s E.3.s add.3.v il.3.v q.3.v o.3.s".split():
            name, i, eng = word.split(".")
            step(name, int(i), eng)
